import numpy as np, ml_dtypes
CORES = [2,3,42,43,82,83,122,123]
N = 8
R, TK = 16, 256
def setup_inputs(rng):
    u = (rng.standard_normal((N, 128, R), dtype=np.float32) / 11).astype(ml_dtypes.bfloat16)
    return {"x": rng.standard_normal((N, 128, TK), dtype=np.float32).astype(ml_dtypes.bfloat16), "u": u, "ut": u.transpose(0, 2, 1).copy(), "vt": rng.standard_normal((N, R, 128), dtype=np.float32).astype(ml_dtypes.bfloat16)}
def setup_inputs_big(rng):
    d = setup_inputs(rng)
    for k in ("x", "u", "ut", "vt"): d[k] = (d[k].astype(np.float32) * 1024.0).astype(d[k].dtype)
    return d
def setup_inputs_small(rng):
    d = setup_inputs(rng)
    for k in ("x", "u", "ut", "vt"): d[k] = (d[k].astype(np.float32) * (1 / 1024.0)).astype(d[k].dtype)
    return d
def setup_inputs_apart(rng):
    d = setup_inputs(rng)
    f = (10.0 ** rng.permutation(np.linspace(-1.5, 1.5, N))).astype(np.float32).reshape(N, 1, 1)
    for k in ("x", "u", "ut", "vt"): d[k] = (d[k].astype(np.float32) * f).astype(d[k].dtype)
    return d
def tie_inputs(x):
    x = dict(x)
    x["ut"] = x["u"].transpose(0, 2, 1).copy()
    return x
def reference(x, u, ut, vt):
    X, U, VT = x.astype(np.float64), u.astype(np.float64), vt.astype(np.float64)
    y = np.stack([sum(VT[j].T @ (U[j].T @ X[r]) for j in range(N)) for r in range(N)])
    return {"y": y.astype(ml_dtypes.bfloat16 if x.dtype != np.float64 else np.float64)}

@@ -1,0 +1,72 @@
+from concourse.bass import DstId, RemoteDMATransfer
+
+N = 8
+R = 16
+D = 128
+TK = 256
+
+SCRATCH = {
+    "G": ("dram", [N, 128, 2 * R * D // 128], "bfloat16"),
+    "F": ("sbuf", [128, 2 * D], "bfloat16"),
+    "xs": ("sbuf", [128, TK], "bfloat16"),
+    "Wp": ("psum", [128, 512], "float32"),
+    "Ws": ("sbuf", [128, D], "bfloat16"),
+    "yp": ("psum", [128, 512], "float32"),
+    "ys": ("sbuf", [128, TK], "bfloat16"),
+}
+SEMAPHORES = ["staged", "xin", "arrived", "sent", "loaded", "mm1", "cp1", "mm2", "cp2", "stored"]
+
+
+def _one_engine_each(core, dsts, topo):
+    used = 0
+    pick = {}
+    for dst in sorted(dsts, key=lambda d: bin(topo.mask(core, d)).count("1")):
+        free = topo.mask(core, dst) & ~used
+        pick[dst] = free & -free
+        used |= pick[dst]
+    return pick
+
+
+def rank_program(g, core, T, topo):
+    rank = T.rank_of(core)
+    if rank is None:
+        return
+    s = T.sem
+    half = 128 // 2
+    others = [c for c in T.cores if c != core]
+    assert all(topo.may_write(core, c) for c in others)
+
+    g.sync.dma_start(T.G[rank, 0:half, :], T.ut[:, :]).then_inc(s.staged, 16)
+    g.scalar.dma_start(T.G[rank, half:128, :], T.vt[:, :]).then_inc(s.staged, 16)
+    g.sync.dma_start(T.xs[:, :], T.x[:, :]).then_inc(s.xin, 16)
+
+    eng = _one_engine_each(core, others, topo)
+    transfers = []
+    for dst in others:
+        rid, pid, _ = topo.addr(dst)
+        transfers.append(RemoteDMATransfer(dst_ids=[DstId(rid=rid, pnc=pid)], dma_engine_mask=eng[dst],
+                                           remote_sem=s.arrived, src=T.G[rank], dst=T.G[rank]))
+    g.wait_ge(s.staged, 32)
+    g.remote_dma_fused(transfers, local_sem=s.sent)
+
+    g.sync.wait_ge(s.staged, 32)
+    g.sync.wait_ge(s.arrived, N - 1)
+    g.sync.dma_start(T.F[:, 0:D], T.G[:, 0:half, :]).then_inc(s.loaded, 16)
+    g.scalar.wait_ge(s.staged, 32)
+    g.scalar.wait_ge(s.arrived, N - 1)
+    g.scalar.dma_start(T.F[:, D:2 * D], T.G[:, half:128, :]).then_inc(s.loaded, 16)
+
+    g.tensor.wait_ge(s.loaded, 32)
+    g.tensor.matmul(T.Wp[:, 0:D], T.F[:, 0:D], T.F[:, D:2 * D], True, True).then_inc(s.mm1, 1)
+    g.vector.wait_ge(s.mm1, 1)
+    g.vector.tensor_copy(T.Ws[:, :], T.Wp[:, 0:D]).then_inc(s.cp1, 1)
+    g.tensor.wait_ge(s.xin, 16)
+    g.tensor.wait_ge(s.cp1, 1)
+    g.tensor.matmul(T.yp[:, 0:TK], T.Ws[:, :], T.xs[:, :], True, True).then_inc(s.mm2, 1)
+    g.vector.wait_ge(s.mm2, 1)
+    g.vector.tensor_copy(T.ys[:, :], T.yp[:, 0:TK]).then_inc(s.cp2, 1)
+
+    g.sync.wait_ge(s.cp2, 1)
+    g.sync.dma_start(T.y[:, :], T.ys[:, :]).then_inc(s.stored, 16)
+    g.sync.wait_ge(s.stored, 16)
+    g.wait_ge(s.sent, N - 1)

@@ -4,69 +4,91 @@ N = 8
 R = 16
 D = 128
 TK = 256
+B = 64
+NW = D // B
+NY = TK // B
 
 SCRATCH = {
     "G": ("dram", [N, 128, 2 * R * D // 128], "bfloat16"),
     "F": ("sbuf", [128, 2 * D], "bfloat16"),
     "xs": ("sbuf", [128, TK], "bfloat16"),
-    "Wp": ("psum", [128, 512], "float32"),
     "Ws": ("sbuf", [128, D], "bfloat16"),
-    "yp": ("psum", [128, 512], "float32"),
     "ys": ("sbuf", [128, TK], "bfloat16"),
 }
-SEMAPHORES = ["staged", "xin", "arrived", "sent", "loaded", "mm1", "cp1", "mm2", "cp2", "stored"]
-
-
-def _one_engine_each(core, dsts, topo):
-    used = 0
-    pick = {}
-    for dst in sorted(dsts, key=lambda d: bin(topo.mask(core, d)).count("1")):
-        free = topo.mask(core, dst) & ~used
-        pick[dst] = free & -free
-        used |= pick[dst]
-    return pick
+for _i in range(NW):
+    SCRATCH["Wp%d" % _i] = ("psum", [128, 512], "float32")
+for _i in range(NY):
+    SCRATCH["yp%d" % _i] = ("psum", [128, 512], "float32")
+SEMAPHORES = (["staged", "xin", "side0", "side1", "sent", "loaded", "cp1", "cp2a", "cp2b", "stored"]
+              + ["mw%d" % _i for _i in range(NW)] + ["my%d" % _i for _i in range(NY)])
 
 
 def rank_program(g, core, T, topo):
-    rank = T.rank_of(core)
-    if rank is None:
+    if T.rank_of(core) is None:
         return
     s = T.sem
     half = 128 // 2
     others = [c for c in T.cores if c != core]
     assert all(topo.may_write(core, c) for c in others)
 
-    g.sync.dma_start(T.G[rank, 0:half, :], T.ut[:, :]).then_inc(s.staged, 16)
-    g.scalar.dma_start(T.G[rank, half:128, :], T.vt[:, :]).then_inc(s.staged, 16)
+    def hops(a, b):
+        ca, cb = topo.chip(a), topo.chip(b)
+        return 0 if ca == cb else 1 if topo.same_plane(ca, cb) or topo.mates(ca, cb) else 2
+
+    def side(c):
+        return hops(T.cores[0], c) // 2
+
+    def order(recv):
+        return sorted(T.cores, key=lambda c: (c != recv, -hops(c, recv)))
+
+    side_sem = [s.side0, s.side1]
+    far = [c for c in others if hops(core, c) == 2]
+    near = sorted((c for c in others if hops(core, c) < 2), key=lambda c: -hops(core, c))
+    assert all(side(c) != side(core) for c in far) and all(side(c) == side(core) for c in near) and len(near) <= len(far)
+
+    g.sync.dma_start(T.G[0, 0:half, :], T.ut[:, :]).then_inc(s.staged, 16)
+    g.scalar.dma_start(T.G[0, half:128, :], T.vt[:, :]).then_inc(s.staged, 16)
+    g.sync.dma_start(T.F[0:R, 0:D], T.ut[:, :]).then_inc(s.loaded, 16)
+    g.scalar.dma_start(T.F[0:R, D:2 * D], T.vt[:, :]).then_inc(s.loaded, 16)
     g.sync.dma_start(T.xs[:, :], T.x[:, :]).then_inc(s.xin, 16)
 
-    eng = _one_engine_each(core, others, topo)
+    common = topo.mask(core, others[0])
+    for c in others:
+        common &= topo.mask(core, c)
+    bits = [1 << b for b in range(common.bit_length()) if common >> b & 1]
     transfers = []
-    for dst in others:
-        rid, pid, _ = topo.addr(dst)
-        transfers.append(RemoteDMATransfer(dst_ids=[DstId(rid=rid, pnc=pid)], dma_engine_mask=eng[dst],
-                                           remote_sem=s.arrived, src=T.G[rank], dst=T.G[rank]))
+    for i, c in enumerate(far):
+        ds = [c] + near[i:i + 1]
+        transfers.append(RemoteDMATransfer(dst_ids=[DstId(rid=topo.addr(d)[0], pnc=topo.addr(d)[1]) for d in ds],
+                                           dma_engine_mask=bits[i * len(bits) // len(far)],
+                                           remote_sem=side_sem[side(core)],
+                                           srcs=[T.G[0]], dsts=[T.G[order(d).index(core)] for d in ds]))
     g.wait_ge(s.staged, 32)
     g.remote_dma_fused(transfers, local_sem=s.sent)
 
-    g.sync.wait_ge(s.staged, 32)
-    g.sync.wait_ge(s.arrived, N - 1)
-    g.sync.dma_start(T.F[:, 0:D], T.G[:, 0:half, :]).then_inc(s.loaded, 16)
-    g.scalar.wait_ge(s.staged, 32)
-    g.scalar.wait_ge(s.arrived, N - 1)
-    g.scalar.dma_start(T.F[:, D:2 * D], T.G[:, half:128, :]).then_inc(s.loaded, 16)
+    waves = [(side_sem[1 - side(core)], 1, 1 + len(far)), (side_sem[side(core)], 1 + len(far), N)]
+    for sem, a, b in waves:
+        g.sync.wait_ge(sem, b - a)
+        g.sync.dma_start(T.F[R * a:R * b, 0:D], T.G[a:b, 0:half, :]).then_inc(s.loaded, 16)
+        g.scalar.wait_ge(sem, b - a)
+        g.scalar.dma_start(T.F[R * a:R * b, D:2 * D], T.G[a:b, half:128, :]).then_inc(s.loaded, 16)
 
-    g.tensor.wait_ge(s.loaded, 32)
-    g.tensor.matmul(T.Wp[:, 0:D], T.F[:, 0:D], T.F[:, D:2 * D], True, True).then_inc(s.mm1, 1)
-    g.vector.wait_ge(s.mm1, 1)
-    g.vector.tensor_copy(T.Ws[:, :], T.Wp[:, 0:D]).then_inc(s.cp1, 1)
+    g.tensor.wait_ge(s.loaded, 16 * 6)
+    for i in range(NW):
+        g.tensor.matmul(T["Wp%d" % i][:, 0:B], T.F[:, 0:D], T.F[:, D + B * i:D + B * (i + 1)], True, True).then_inc(s["mw%d" % i], 1)
+        g.vector.wait_ge(s["mw%d" % i], 1)
+        g.vector.tensor_copy(T.Ws[:, B * i:B * (i + 1)], T["Wp%d" % i][:, 0:B]).then_inc(s.cp1, 1)
     g.tensor.wait_ge(s.xin, 16)
-    g.tensor.wait_ge(s.cp1, 1)
-    g.tensor.matmul(T.yp[:, 0:TK], T.Ws[:, :], T.xs[:, :], True, True).then_inc(s.mm2, 1)
-    g.vector.wait_ge(s.mm2, 1)
-    g.vector.tensor_copy(T.ys[:, :], T.yp[:, 0:TK]).then_inc(s.cp2, 1)
+    g.tensor.wait_ge(s.cp1, NW)
+    h = NY // 2
+    for i in range(NY):
+        g.tensor.matmul(T["yp%d" % i][:, 0:B], T.Ws[:, :], T.xs[:, B * i:B * (i + 1)], True, True).then_inc(s["my%d" % i], 1)
+        g.vector.wait_ge(s["my%d" % i], 1)
+        g.vector.tensor_copy(T.ys[:, B * i:B * (i + 1)], T["yp%d" % i][:, 0:B]).then_inc(s.cp2a if i < h else s.cp2b, 1)
 
-    g.sync.wait_ge(s.cp2, 1)
-    g.sync.dma_start(T.y[:, :], T.ys[:, :]).then_inc(s.stored, 16)
-    g.sync.wait_ge(s.stored, 16)
-    g.wait_ge(s.sent, N - 1)
+    g.scalar.wait_ge(s.cp2a, h)
+    g.scalar.dma_start(T.y[:, 0:B * h], T.ys[:, 0:B * h]).then_inc(s.stored, 16)
+    g.sync.wait_ge(s.cp2b, NY - h)
+    g.sync.dma_start(T.y[:, B * h:TK], T.ys[:, B * h:TK]).then_inc(s.stored, 16)
+    g.sync.wait_ge(s.stored, 32)
+    g.wait_ge(s.sent, len(transfers))

from concourse.bass import DstId, RemoteDMATransfer

N = 8
R = 16
D = 128
TK = 256
B = 64
NW = D // B
NY = TK // B

SCRATCH = {
    "G": ("dram", [N, 128, 2 * R * D // 128], "bfloat16"),
    "F": ("sbuf", [128, 2 * D], "bfloat16"),
    "xs": ("sbuf", [128, TK], "bfloat16"),
    "Ws": ("sbuf", [128, D], "bfloat16"),
    "ys": ("sbuf", [128, TK], "bfloat16"),
}
for _i in range(NW):
    SCRATCH["Wp%d" % _i] = ("psum", [128, 512], "float32")
for _i in range(NY):
    SCRATCH["yp%d" % _i] = ("psum", [128, 512], "float32")
SEMAPHORES = (["staged", "xin", "side0", "side1", "sent", "loaded", "cp1", "cp2a", "cp2b", "stored"]
              + ["mw%d" % _i for _i in range(NW)] + ["my%d" % _i for _i in range(NY)])


def rank_program(g, core, T, topo):
    if T.rank_of(core) is None:
        return
    s = T.sem
    half = 128 // 2
    others = [c for c in T.cores if c != core]
    assert all(topo.may_write(core, c) for c in others)

    def hops(a, b):
        ca, cb = topo.chip(a), topo.chip(b)
        return 0 if ca == cb else 1 if topo.same_plane(ca, cb) or topo.mates(ca, cb) else 2

    def side(c):
        return hops(T.cores[0], c) // 2

    def order(recv):
        return sorted(T.cores, key=lambda c: (c != recv, -hops(c, recv)))

    side_sem = [s.side0, s.side1]
    far = [c for c in others if hops(core, c) == 2]
    near = sorted((c for c in others if hops(core, c) < 2), key=lambda c: -hops(core, c))
    assert all(side(c) != side(core) for c in far) and all(side(c) == side(core) for c in near) and len(near) <= len(far)

    g.sync.dma_start(T.G[0, 0:half, :], T.ut[:, :]).then_inc(s.staged, 16)
    g.scalar.dma_start(T.G[0, half:128, :], T.vt[:, :]).then_inc(s.staged, 16)
    g.sync.dma_start(T.F[0:R, 0:D], T.ut[:, :]).then_inc(s.loaded, 16)
    g.scalar.dma_start(T.F[0:R, D:2 * D], T.vt[:, :]).then_inc(s.loaded, 16)
    g.sync.dma_start(T.xs[:, :], T.x[:, :]).then_inc(s.xin, 16)

    common = topo.mask(core, others[0])
    for c in others:
        common &= topo.mask(core, c)
    bits = [1 << b for b in range(common.bit_length()) if common >> b & 1]
    transfers = []
    for i, c in enumerate(far):
        ds = [c] + near[i:i + 1]
        transfers.append(RemoteDMATransfer(dst_ids=[DstId(rid=topo.addr(d)[0], pnc=topo.addr(d)[1]) for d in ds],
                                           dma_engine_mask=bits[i * len(bits) // len(far)],
                                           remote_sem=side_sem[side(core)],
                                           srcs=[T.G[0]], dsts=[T.G[order(d).index(core)] for d in ds]))
    g.wait_ge(s.staged, 32)
    g.remote_dma_fused(transfers, local_sem=s.sent)

    waves = [(side_sem[1 - side(core)], 1, 1 + len(far)), (side_sem[side(core)], 1 + len(far), N)]
    for sem, a, b in waves:
        g.sync.wait_ge(sem, b - a)
        g.sync.dma_start(T.F[R * a:R * b, 0:D], T.G[a:b, 0:half, :]).then_inc(s.loaded, 16)
        g.scalar.wait_ge(sem, b - a)
        g.scalar.dma_start(T.F[R * a:R * b, D:2 * D], T.G[a:b, half:128, :]).then_inc(s.loaded, 16)

    g.tensor.wait_ge(s.loaded, 16 * 6)
    for i in range(NW):
        g.tensor.matmul(T["Wp%d" % i][:, 0:B], T.F[:, 0:D], T.F[:, D + B * i:D + B * (i + 1)], True, True).then_inc(s["mw%d" % i], 1)
        g.vector.wait_ge(s["mw%d" % i], 1)
        g.vector.tensor_copy(T.Ws[:, B * i:B * (i + 1)], T["Wp%d" % i][:, 0:B]).then_inc(s.cp1, 1)
    g.tensor.wait_ge(s.xin, 16)
    g.tensor.wait_ge(s.cp1, NW)
    h = NY // 2
    for i in range(NY):
        g.tensor.matmul(T["yp%d" % i][:, 0:B], T.Ws[:, :], T.xs[:, B * i:B * (i + 1)], True, True).then_inc(s["my%d" % i], 1)
        g.vector.wait_ge(s["my%d" % i], 1)
        g.vector.tensor_copy(T.ys[:, B * i:B * (i + 1)], T["yp%d" % i][:, 0:B]).then_inc(s.cp2a if i < h else s.cp2b, 1)

    g.scalar.wait_ge(s.cp2a, h)
    g.scalar.dma_start(T.y[:, 0:B * h], T.ys[:, 0:B * h]).then_inc(s.stored, 16)
    g.sync.wait_ge(s.cp2b, NY - h)
    g.sync.dma_start(T.y[:, B * h:TK], T.ys[:, B * h:TK]).then_inc(s.stored, 16)
    g.sync.wait_ge(s.stored, 32)
    g.wait_ge(s.sent, len(transfers))
